import numpy as np
import ml_dtypes


def mxq(x, axis, fmt="e4m3"):
    dtype, down = {"e4m3": (ml_dtypes.float8_e4m3fn, 7), "e5m2": (ml_dtypes.float8_e5m2, 14)}[fmt]
    v = np.moveaxis(np.asarray(x, np.float32).astype(ml_dtypes.bfloat16).astype(np.float64), axis, -1)
    blocks = v.reshape(v.shape[:-1] + (-1, 32))
    amax = np.abs(blocks).max(-1, keepdims=True)
    byte = np.maximum(np.where(amax > 0, np.frexp(amax)[1] - 1 + 127, 0) - down, 1)
    scale = np.exp2(byte - 127.0)
    codes = (blocks / scale).astype(np.float32).astype(dtype).astype(np.float64)
    return np.moveaxis((codes * scale).reshape(v.shape), -1, axis)


WIDE = False


def mx_kscale(k):
    if not WIDE:
        return np.ones(k)
    levels = np.array([10, -10, 5, -5, 0])
    if k % 512:
        return np.exp2(np.random.permutation(np.resize(levels, k // 32))).repeat(32)
    a = np.empty((k // 512, 16))
    for p in range(k // 512):
        a[p, :8] = np.random.permutation(np.resize(levels, 8))
        for g in range(8):
            far = levels[np.abs(levels - a[p, g]) >= 10]
            a[p, g + 8] = far[np.random.randint(len(far))]
    return np.exp2(a.ravel()).repeat(32)


BF16 = ml_dtypes.bfloat16


def bf(x):
    return np.asarray(x, np.float32).astype(BF16)


def f64(x):
    return np.asarray(x).astype(np.float64)


T, J, K, N = 2048, 512, 512, 1024


def draw0():
    u, v = mx_kscale(J), mx_kscale(K)
    return {
        "t": bf(np.random.uniform(-1.0, 1.0, T)),
        "s": bf(np.random.uniform(-1.5, 1.0, J)),
        "rho": bf(np.random.standard_normal(J) * u),
        "delta": bf(np.random.standard_normal((J, N)) * (2.0 / np.sqrt(J)) / u[:, None]),
        "omega": bf(np.random.uniform(-3.0, 3.0, K)),
        "amp": bf((1.0 + 0.2 * np.random.standard_normal(K)) * v),
        "beta": bf(np.random.standard_normal((K, N)) * (1.5 / np.sqrt(K)) / v[:, None]),
    }


def hinge_features(t, s, rho):
    return rho[None, :] * np.maximum(t[:, None] - s[None, :], 0.0)


def sine_features(t, omega, amp):
    return amp[None, :] * np.sin(omega[None, :] * t[:, None])


def core(t, s, rho, delta, omega, amp, beta):
    a = hinge_features(f64(t), f64(s), f64(rho))
    trend = mxq(a, 1, "e4m3") @ mxq(f64(delta), 0, "e4m3")
    f = sine_features(f64(t), f64(omega), f64(amp))
    season = mxq(f, 1, "e4m3") @ mxq(f64(beta), 0, "e4m3")
    return trend * (1.0 + season)


def e4m3fn_bytes(y):
    return np.clip(np.asarray(y, np.float64), -448.0, 448.0).astype(np.float32).astype(ml_dtypes.float8_e4m3fn).view(np.uint8)


def e4m3fn_values(b):
    return np.asarray(b, np.uint8).view(ml_dtypes.float8_e4m3fn).astype(np.float64)


def setup_inputs():
    d = draw0()
    x0 = np.asarray(d['delta']).astype(np.float64)
    s = (np.max(np.abs(x0), axis=(1,), keepdims=True) / 448.0).astype(np.float32)
    out = {}
    for k, v in d.items():
        if k == 'delta':
            out['delta_bytes'] = e4m3fn_bytes(x0 / s.astype(np.float64))
            out['delta_scale'] = s
        else:
            out[k] = v
    return out


def reference(t, s, rho, delta_bytes, delta_scale, omega, amp, beta):
    return core(t, s, rho, e4m3fn_values(delta_bytes) * delta_scale.astype(np.float64), omega, amp, beta)

@@ -1,0 +1,298 @@
+from contextlib import ExitStack
+
+import concourse.mybir as mybir
+
+T, K, N = 2048, 512, 1024
+FLOPS = 2 * 2 * T * K * N
+
+F32 = mybir.dt.float32
+BF16 = mybir.dt.bfloat16
+U32 = mybir.dt.uint32
+U8 = mybir.dt.uint8
+FP8 = mybir.dt.float8_e4m3fn
+FP8X4 = mybir.dt.float8_e4m3fn_x4
+ALU = mybir.AluOpType
+ACT = mybir.ActivationFunctionType
+
+P = 128
+PACK = 4
+HALF = 512
+TIME_ROW = 64
+CHUNK_TILES = (2, 3, 4, 4, 3)
+LEAD = 2
+EARLY_TILES = 5
+ONE_PAIR = 0x3F803F80
+MINUS_ONE_PAIR = 0xBF80BF80
+
+
+def tile_changepointtrendtimeslearnedsines_kernel(
+    tc, t, s, rho, delta_bytes, delta_scale, omega, amp, beta, out
+):
+    nc = tc.nc
+    n_chunks = len(CHUNK_TILES)
+    first_tile = [sum(CHUNK_TILES[:c]) for c in range(n_chunks)]
+    chunk_of = [c for c in range(n_chunks) for unused in range(CHUNK_TILES[c])]
+
+    with ExitStack() as ctx:
+        keep = ctx.enter_context(tc.tile_pool(name="keep", bufs=1))
+        work = ctx.enter_context(tc.tile_pool(name="work", bufs=1))
+        psum = ctx.enter_context(tc.psum_pool(name="psum", bufs=1))
+        ctx.enter_context(tc.manual_schedule())
+
+        early = EARLY_TILES * P
+        moving_early = keep.tile([P, early], BF16, name="moving_early")
+        moving_late = keep.tile([P, T - early], BF16, name="moving_late")
+        stationary = keep.tile([P, (PACK + 1) * P], BF16, name="stationary")
+        nc.vector.memset(moving_early[:].bitcast(U32), MINUS_ONE_PAIR)
+        nc.vector.memset(stationary[:].bitcast(U32), 0)
+        nc.vector.memset(stationary[TIME_ROW : TIME_ROW + 1, :].bitcast(U32), ONE_PAIR)
+        nc.vector.memset(moving_late[:].bitcast(U32), MINUS_ONE_PAIR)
+
+        def moving(lo, hi):
+            return moving_early[:, lo:hi] if hi <= early else moving_late[:, lo - early : hi - early]
+
+        s_row = keep.tile([1, K], BF16, name="s_row")
+        omega_bf = keep.tile([P, PACK], BF16, name="omega_bf")
+        rho_bf = keep.tile([P, PACK], BF16, name="rho_bf")
+        amp_bf = keep.tile([P, PACK], BF16, name="amp_bf")
+        scale = keep.tile([P, PACK], F32, name="scale")
+        delta_raw = keep.tile([P, PACK, N], U8, name="delta_raw")
+        t_row = t.rearrange("(o i) -> o i", o=1)
+        beta_raw = []
+        for h in range(2):
+            raw = keep.tile([P, PACK, HALF], BF16, name="beta_raw%d" % h)
+            beta_raw.append(raw)
+
+        def load_beta(h):
+            nc.sync.dma_start(
+                out=beta_raw[h][:], in_=beta[:, h * HALF : (h + 1) * HALF].rearrange("(p j) n -> p j n", j=PACK)
+            )
+
+        nc.scalar.dma_start(out=s_row[:], in_=s.rearrange("(o k) -> o k", o=1))
+        nc.scalar.dma_start(out=omega_bf[:], in_=omega.rearrange("(p j) -> p j", j=PACK))
+        nc.sync.dma_start(out=scale[:], in_=delta_scale.rearrange("(p j) o -> p (j o)", j=PACK))
+        nc.sync.dma_start(out=moving_early[TIME_ROW : TIME_ROW + 1, :], in_=t_row[:, :early])
+        nc.sync.dma_start(out=delta_raw[:], in_=delta_bytes.rearrange("(p j) n -> p j n", j=PACK))
+        load_beta(0)
+        nc.sync.dma_start(out=rho_bf[:], in_=rho.rearrange("(p j) -> p j", j=PACK))
+        nc.sync.dma_start(out=amp_bf[:], in_=amp.rearrange("(p j) -> p j", j=PACK))
+        nc.sync.dma_start(out=moving_late[TIME_ROW : TIME_ROW + 1, :], in_=t_row[:, early:])
+        load_beta(1)
+
+        omega_f32 = keep.tile([P, PACK], F32, name="omega_f32")
+        amp_f32 = keep.tile([P, PACK], F32, name="amp_f32")
+        nc.vector.tensor_copy(out=omega_f32[:], in_=omega_bf[:])
+        nc.vector.tensor_copy(
+            out=stationary[0:1, : PACK * P].rearrange("o (j m) -> o j m", j=PACK),
+            in_=s_row[:].rearrange("o (m j) -> o j m", j=PACK),
+        )
+        scale_run = keep.tile([P, P * PACK], F32, name="scale_run")
+        nc.vector.tensor_copy(
+            out=scale_run[:].rearrange("p (n j) -> p n j", j=PACK),
+            in_=scale[:].unsqueeze(1).to_broadcast([P, P, PACK]),
+        )
+
+        grouped = {}
+        quantised = {}
+        sines = {}
+        times = {}
+        banks = {}
+        trend_sb = {}
+
+        def grouped_tile(key, width, pool, tag):
+            grouped[key] = pool.tile([P, width * PACK], BF16, name="grouped_%s%d" % key, tag=tag, align_bytes=64)
+            return grouped[key][:].rearrange("p (n j) -> p n j", j=PACK)
+
+        def quantise(key):
+            width = grouped[key].shape[1] // PACK
+            codes = keep.tile([P, width], U32, name="codes_%s%d" % key, align_bytes=64)
+            scales = keep.tile([P, width], U8, name="scales_%s%d" % key, align_bytes=64)
+            nc.vector.quantize_mx(out=codes[:].bitcast(FP8X4), scales=scales[:], in_=grouped[key][:])
+            quantised[key] = (codes, scales)
+
+        def interleave(engine_copy, key, planes):
+            dst = grouped_tile(key, HALF, keep, "grouped_%s%d" % key)
+            engine_copy(
+                out=dst.rearrange("p (c i) j -> p c j i", i=4),
+                in_=planes[:].rearrange("p j (c i) -> p c j i", i=4),
+            )
+
+        def sine_plane(c, j):
+            width = CHUNK_TILES[c] * P
+            if j == 0:
+                times[c] = psum.tile([P, HALF], F32, name="times", tag="times", bufs=1)
+                lo = first_tile[c] * P
+                nc.tensor.matmul(
+                    times[c][:, :width], lhsT=stationary[:, PACK * P :], rhs=moving(lo, lo + width), start=True, stop=True
+                )
+                sines[c] = work.tile([P, PACK, width], F32, name="sines", tag="sines", bufs=2)
+            nc.scalar.activation(
+                out=sines[c][:, j, :], in_=times[c][:, :width], func=ACT.Sin, scale=omega_f32[:, j : j + 1]
+            )
+
+        def amplitude(c):
+            width = CHUNK_TILES[c] * P
+            dst = grouped_tile(("f", c), width, work, "grouped_f")
+            nc.gpsimd.tensor_tensor(
+                out=dst,
+                in0=sines[c][:].rearrange("p j i -> p i j"),
+                in1=amp_f32[:].unsqueeze(1).to_broadcast([P, width, PACK]),
+                op=ALU.mult,
+            )
+
+        def new_bank(key):
+            banks[key] = psum.tile([P, HALF], F32, name="bank", tag="bank", bufs=7)
+            return banks[key]
+
+        def differences(g):
+            bank = new_bank(("hinge", g))
+            planes = bank[:].rearrange("p (i j) -> p j i", j=PACK)
+            for j in range(PACK):
+                nc.tensor.matmul(
+                    planes[:, j, :],
+                    lhsT=stationary[:, j * P : (j + 1) * P],
+                    rhs=moving(g * P, (g + 1) * P),
+                    start=True,
+                    stop=True,
+                )
+
+        def hinge(g):
+            c = chunk_of[g]
+            if g == first_tile[c]:
+                grouped_tile(("a", c), CHUNK_TILES[c] * P, keep, "grouped_a%d" % c)
+            lo = (g - first_tile[c]) * P * PACK
+            nc.vector.scalar_tensor_tensor(
+                out=grouped[("a", c)][:, lo : lo + P * PACK].rearrange("p (i j) -> p i j", j=PACK),
+                in0=banks[("hinge", g)][:].rearrange("p (i j) -> p i j", j=PACK),
+                scalar=0.0,
+                in1=rho_bf[:].unsqueeze(1).to_broadcast([P, P, PACK]),
+                op0=ALU.max,
+                op1=ALU.mult,
+            )
+
+        def product(name, feature, weight, g, h):
+            c = chunk_of[g]
+            cols = slice((g - first_tile[c]) * P, (g - first_tile[c] + 1) * P)
+            codes, scales = quantised[(feature, c)]
+            w_codes, w_scales = quantised[(weight, h)]
+            bank = new_bank((name, g, h))
+            nc.tensor.matmul_mx(
+                bank[:],
+                lhsT=codes[:, cols].bitcast(FP8X4),
+                lhsT_scale=scales[:, cols],
+                rhs=w_codes[:].bitcast(FP8X4),
+                rhs_scale=w_scales[:],
+                start=True,
+                stop=True,
+            )
+            return bank
+
+        def trend(g, h):
+            bank = product("trend", "a", "delta", g, h)
+            trend_sb[(g, h)] = work.tile([P, HALF], F32, name="trend_sb", tag="trend_sb", bufs=4)
+            nc.scalar.copy(out=trend_sb[(g, h)][:], in_=bank[:])
+
+        def season(g, h):
+            product("season", "f", "beta", g, h)
+
+        def finish(g, h):
+            result = work.tile([P, HALF], F32, name="result", tag="result", bufs=6)
+            nc.vector.scalar_tensor_tensor(
+                out=result[:],
+                in0=banks[("season", g, h)][:],
+                scalar=1.0,
+                in1=trend_sb[(g, h)][:],
+                op0=ALU.add,
+                op1=ALU.mult,
+            )
+            nc.sync.dma_start(out=out[g * P : (g + 1) * P, h * HALF : (h + 1) * HALF], in_=result[:])
+
+        for j in range(PACK):
+            sine_plane(0, j)
+        for g in range(5):
+            differences(g)
+        grouped_tile(("delta", 0), HALF, keep, "grouped_delta0")
+        for lo in range(0, HALF, P):
+            nc.vector.tensor_tensor(
+                out=grouped[("delta", 0)][:, lo * PACK : (lo + P) * PACK].rearrange("p (n j) -> p n j", j=PACK),
+                in0=delta_raw[:, :, lo : lo + P].bitcast(FP8).rearrange("p j n -> p n j"),
+                in1=scale_run[:].rearrange("p (n j) -> p n j", j=PACK),
+                op=ALU.mult,
+            )
+        nc.vector.tensor_copy(out=amp_f32[:], in_=amp_bf[:])
+        amplitude(0)
+        interleave(nc.scalar.copy, ("beta", 0), beta_raw[0])
+        for j in range(PACK):
+            sine_plane(1, j)
+        delta_planes = keep.tile([P, PACK, HALF], BF16, name="delta_planes")
+        for j in range(PACK):
+            nc.scalar.activation(
+                out=delta_planes[:, j, :],
+                in_=delta_raw[:, j, HALF:N].bitcast(FP8),
+                func=ACT.Copy,
+                scale=scale[:, j : j + 1],
+            )
+
+        def outs(c):
+            return [("out", g, h) for g in range(first_tile[c], first_tile[c] + CHUNK_TILES[c]) for h in range(2)]
+
+        def hinges(lo, hi):
+            return [("hinge", g) for g in range(lo, hi)]
+
+        def features(c):
+            return [("quantise", "a", c), ("quantise", "f", c)]
+
+        o1, o2, o3, o4 = outs(1), outs(2), outs(3), outs(4)
+        steps = (
+            hinges(0, 5)
+            + [("quantise", "delta", 0), ("quantise", "beta", 0)]
+            + features(0)
+            + hinges(5, 8) + [("out", 0, 0)] + hinges(8, 9) + [("out", 1, 0)] + hinges(9, 11)
+            + [("interleave", "delta", 1), ("quantise", "a", 1), ("quantise", "delta", 1), ("quantise", "beta", 1), ("quantise", "f", 1)]
+            + [("out", 0, 1), ("out", 1, 1)] + o1[:2] + hinges(11, 12) + o1[2:4] + hinges(12, 13) + o1[4:]
+            + features(2)
+            + hinges(13, 14) + o2[:4] + hinges(14, 15) + o2[4:]
+            + features(3)
+            + hinges(15, 16) + o3[:-1]
+            + features(4)
+            + o3[-1:] + o4
+        )
+        side = {
+            ("hinge", 8): [lambda: interleave(nc.scalar.copy, ("beta", 1), beta_raw[1])],
+            ("hinge", 9): [lambda: [sine_plane(2, j) for j in range(PACK)]],
+            ("hinge", 11): [lambda: sine_plane(3, 0)],
+            ("hinge", 12): [lambda: sine_plane(3, 1)],
+            ("quantise", "a", 2): [lambda: [sine_plane(3, j) for j in (2, 3)]],
+            ("hinge", 13): [lambda: sine_plane(4, 0)],
+            ("hinge", 14): [lambda: sine_plane(4, 1)],
+            ("quantise", "a", 3): [lambda: [sine_plane(4, j) for j in (2, 3)]],
+        }
+
+        def prepare(step):
+            if step[0] == "hinge":
+                if step not in banks:
+                    differences(step[1])
+            if step[0] == "out":
+                g, h = step[1:]
+                c = chunk_of[g]
+                if (g, h) not in trend_sb and ("a", c) in quantised and ("delta", h) in quantised:
+                    trend(g, h)
+                if ("season", g, h) not in banks and ("f", c) in quantised and ("beta", h) in quantised:
+                    season(g, h)
+
+        for k, step in enumerate(steps):
+            for job in side.get(step, []):
+                job()
+            ahead = [later for later in steps[k + 1 :] if later[0] in ("hinge", "out")][:LEAD]
+            for later in [step] + ahead:
+                prepare(later)
+            if step[0] == "hinge":
+                hinge(step[1])
+            elif step[0] == "out":
+                finish(step[1], step[2])
+            elif step[0] == "interleave":
+                interleave(nc.vector.tensor_copy, step[1:], delta_planes)
+            else:
+                quantise(step[1:])
+                if step[1] == "f" and step[2] + 1 < n_chunks:
+                    amplitude(step[2] + 1)

@@ -20,6 +20,7 @@ HALF = 512
 TIME_ROW = 64
 CHUNK_TILES = (2, 3, 4, 4, 3)
 LEAD = 2
+TREND_LEAD = 4
 EARLY_TILES = 5
 ONE_PAIR = 0x3F803F80
 MINUS_ONE_PAIR = 0xBF80BF80
@@ -56,12 +57,20 @@ def tile_changepointtrendtimeslearnedsines_kernel(
         rho_bf = keep.tile([P, PACK], BF16, name="rho_bf")
         amp_bf = keep.tile([P, PACK], BF16, name="amp_bf")
         scale = keep.tile([P, PACK], F32, name="scale")
-        delta_raw = keep.tile([P, PACK, N], U8, name="delta_raw")
         t_row = t.rearrange("(o i) -> o i", o=1)
         beta_raw = []
+        delta_raw = []
         for h in range(2):
             raw = keep.tile([P, PACK, HALF], BF16, name="beta_raw%d" % h)
             beta_raw.append(raw)
+            raw_bytes = keep.tile([P, PACK, HALF], U8, name="delta_raw%d" % h)
+            delta_raw.append(raw_bytes)
+
+        def load_delta(h):
+            nc.sync.dma_start(
+                out=delta_raw[h][:],
+                in_=delta_bytes[:, h * HALF : (h + 1) * HALF].rearrange("(p j) n -> p j n", j=PACK),
+            )
 
         def load_beta(h):
             nc.sync.dma_start(
@@ -70,13 +79,14 @@ def tile_changepointtrendtimeslearnedsines_kernel(
 
         nc.scalar.dma_start(out=s_row[:], in_=s.rearrange("(o k) -> o k", o=1))
         nc.scalar.dma_start(out=omega_bf[:], in_=omega.rearrange("(p j) -> p j", j=PACK))
+        nc.scalar.dma_start(out=rho_bf[:], in_=rho.rearrange("(p j) -> p j", j=PACK))
+        nc.scalar.dma_start(out=amp_bf[:], in_=amp.rearrange("(p j) -> p j", j=PACK))
         nc.sync.dma_start(out=scale[:], in_=delta_scale.rearrange("(p j) o -> p (j o)", j=PACK))
         nc.sync.dma_start(out=moving_early[TIME_ROW : TIME_ROW + 1, :], in_=t_row[:, :early])
-        nc.sync.dma_start(out=delta_raw[:], in_=delta_bytes.rearrange("(p j) n -> p j n", j=PACK))
+        load_delta(0)
         load_beta(0)
-        nc.sync.dma_start(out=rho_bf[:], in_=rho.rearrange("(p j) -> p j", j=PACK))
-        nc.sync.dma_start(out=amp_bf[:], in_=amp.rearrange("(p j) -> p j", j=PACK))
         nc.sync.dma_start(out=moving_late[TIME_ROW : TIME_ROW + 1, :], in_=t_row[:, early:])
+        load_delta(1)
         load_beta(1)
 
         omega_f32 = keep.tile([P, PACK], F32, name="omega_f32")
@@ -120,7 +130,7 @@ def tile_changepointtrendtimeslearnedsines_kernel(
         def sine_plane(c, j):
             width = CHUNK_TILES[c] * P
             if j == 0:
-                times[c] = psum.tile([P, HALF], F32, name="times", tag="times", bufs=1)
+                times[c] = psum.tile([P, HALF], F32, name="times", tag="scalar_bank", bufs=3)
                 lo = first_tile[c] * P
                 nc.tensor.matmul(
                     times[c][:, :width], lhsT=stationary[:, PACK * P :], rhs=moving(lo, lo + width), start=True, stop=True
@@ -134,14 +144,17 @@ def tile_changepointtrendtimeslearnedsines_kernel(
             width = CHUNK_TILES[c] * P
             dst = grouped_tile(("f", c), width, work, "grouped_f")
             nc.gpsimd.tensor_tensor(
-                out=dst,
-                in0=sines[c][:].rearrange("p j i -> p i j"),
-                in1=amp_f32[:].unsqueeze(1).to_broadcast([P, width, PACK]),
+                out=dst.rearrange("p (c i) j -> p c j i", i=4),
+                in0=sines[c][:].rearrange("p j (c i) -> p c j i", i=4),
+                in1=amp_f32[:].unsqueeze(1).unsqueeze(3).to_broadcast([P, width // 4, PACK, 4]),
                 op=ALU.mult,
             )
 
         def new_bank(key):
-            banks[key] = psum.tile([P, HALF], F32, name="bank", tag="bank", bufs=7)
+            if key[0] == "trend":
+                banks[key] = psum.tile([P, HALF], F32, name="bank", tag="scalar_bank", bufs=3)
+            else:
+                banks[key] = psum.tile([P, HALF], F32, name="bank", tag="vector_bank", bufs=5)
             return banks[key]
 
         def differences(g):
@@ -189,7 +202,7 @@ def tile_changepointtrendtimeslearnedsines_kernel(
 
         def trend(g, h):
             bank = product("trend", "a", "delta", g, h)
-            trend_sb[(g, h)] = work.tile([P, HALF], F32, name="trend_sb", tag="trend_sb", bufs=4)
+            trend_sb[(g, h)] = work.tile([P, HALF], F32, name="trend_sb", tag="trend_sb", bufs=TREND_LEAD + 2)
             nc.scalar.copy(out=trend_sb[(g, h)][:], in_=bank[:])
 
         def season(g, h):
@@ -207,31 +220,31 @@ def tile_changepointtrendtimeslearnedsines_kernel(
             )
             nc.sync.dma_start(out=out[g * P : (g + 1) * P, h * HALF : (h + 1) * HALF], in_=result[:])
 
-        for j in range(PACK):
-            sine_plane(0, j)
-        for g in range(5):
-            differences(g)
-        grouped_tile(("delta", 0), HALF, keep, "grouped_delta0")
-        for lo in range(0, HALF, P):
-            nc.vector.tensor_tensor(
-                out=grouped[("delta", 0)][:, lo * PACK : (lo + P) * PACK].rearrange("p (n j) -> p n j", j=PACK),
-                in0=delta_raw[:, :, lo : lo + P].bitcast(FP8).rearrange("p j n -> p n j"),
-                in1=scale_run[:].rearrange("p (n j) -> p n j", j=PACK),
-                op=ALU.mult,
-            )
-        nc.vector.tensor_copy(out=amp_f32[:], in_=amp_bf[:])
-        amplitude(0)
-        interleave(nc.scalar.copy, ("beta", 0), beta_raw[0])
-        for j in range(PACK):
-            sine_plane(1, j)
+        def widen_first_half():
+            grouped_tile(("delta", 0), HALF, keep, "grouped_delta0")
+            for lo in range(0, HALF, P):
+                nc.vector.tensor_tensor(
+                    out=grouped[("delta", 0)][:, lo * PACK : (lo + P) * PACK].rearrange("p (n j) -> p n j", j=PACK),
+                    in0=delta_raw[0][:, :, lo : lo + P].bitcast(FP8).rearrange("p j n -> p n j"),
+                    in1=scale_run[:].rearrange("p (n j) -> p n j", j=PACK),
+                    op=ALU.mult,
+                )
+            nc.vector.tensor_copy(out=amp_f32[:], in_=amp_bf[:])
+            amplitude(0)
+
         delta_planes = keep.tile([P, PACK, HALF], BF16, name="delta_planes")
-        for j in range(PACK):
-            nc.scalar.activation(
-                out=delta_planes[:, j, :],
-                in_=delta_raw[:, j, HALF:N].bitcast(FP8),
-                func=ACT.Copy,
-                scale=scale[:, j : j + 1],
-            )
+
+        def widen_second_half():
+            for j in range(PACK):
+                nc.scalar.activation(
+                    out=delta_planes[:, j, :],
+                    in_=delta_raw[1][:, j, :].bitcast(FP8),
+                    func=ACT.Copy,
+                    scale=scale[:, j : j + 1],
+                )
+
+        def sine_planes(c, planes):
+            return lambda: [sine_plane(c, j) for j in planes]
 
         def outs(c):
             return [("out", g, h) for g in range(first_tile[c], first_tile[c] + CHUNK_TILES[c]) for h in range(2)]
@@ -239,36 +252,37 @@ def tile_changepointtrendtimeslearnedsines_kernel(
         def hinges(lo, hi):
             return [("hinge", g) for g in range(lo, hi)]
 
-        def features(c):
-            return [("quantise", "a", c), ("quantise", "f", c)]
+        def q(*keys):
+            return [("quantise",) + key for key in keys]
 
         o1, o2, o3, o4 = outs(1), outs(2), outs(3), outs(4)
         steps = (
-            hinges(0, 5)
-            + [("quantise", "delta", 0), ("quantise", "beta", 0)]
-            + features(0)
-            + hinges(5, 8) + [("out", 0, 0)] + hinges(8, 9) + [("out", 1, 0)] + hinges(9, 11)
-            + [("interleave", "delta", 1), ("quantise", "a", 1), ("quantise", "delta", 1), ("quantise", "beta", 1), ("quantise", "f", 1)]
-            + [("out", 0, 1), ("out", 1, 1)] + o1[:2] + hinges(11, 12) + o1[2:4] + hinges(12, 13) + o1[4:]
-            + features(2)
-            + hinges(13, 14) + o2[:4] + hinges(14, 15) + o2[4:]
-            + features(3)
-            + hinges(15, 16) + o3[:-1]
-            + features(4)
+            [("widen",)] + hinges(0, 5)
+            + q(("delta", 0), ("a", 0), ("beta", 0), ("a", 1), ("f", 0))
+            + hinges(5, 7) + [("out", 0, 0)] + hinges(7, 9) + [("out", 1, 0)] + hinges(9, 11)
+            + q(("a", 2), ("delta", 1), ("beta", 1), ("f", 1))
+            + hinges(11, 13) + [("out", 0, 1), ("out", 1, 1)] + o1
+            + q(("a", 3), ("f", 2))
+            + hinges(13, 14) + o2[:3] + hinges(14, 15) + o2[3:6] + hinges(15, 16) + o2[6:7]
+            + q(("a", 4), ("f", 3))
+            + o2[7:] + o3[:-1]
+            + q(("f", 4))
             + o3[-1:] + o4
         )
         side = {
-            ("hinge", 8): [lambda: interleave(nc.scalar.copy, ("beta", 1), beta_raw[1])],
-            ("hinge", 9): [lambda: [sine_plane(2, j) for j in range(PACK)]],
-            ("hinge", 11): [lambda: sine_plane(3, 0)],
-            ("hinge", 12): [lambda: sine_plane(3, 1)],
-            ("quantise", "a", 2): [lambda: [sine_plane(3, j) for j in (2, 3)]],
-            ("hinge", 13): [lambda: sine_plane(4, 0)],
-            ("hinge", 14): [lambda: sine_plane(4, 1)],
-            ("quantise", "a", 3): [lambda: [sine_plane(4, j) for j in (2, 3)]],
+            ("widen",): [sine_planes(0, range(PACK))],
+            ("hinge", 0): [lambda: interleave(nc.scalar.copy, ("beta", 0), beta_raw[0]), sine_planes(1, range(PACK)), widen_second_half],
+            ("hinge", 5): [lambda: interleave(nc.scalar.copy, ("delta", 1), delta_planes)],
+            ("hinge", 7): [lambda: interleave(nc.scalar.copy, ("beta", 1), beta_raw[1])],
+            ("hinge", 9): [sine_planes(2, range(PACK))],
+            ("out", 2, 1): [sine_planes(3, (0,))],
+            ("out", 3, 0): [sine_planes(3, (1,))],
+            ("out", 4, 0): [sine_planes(3, (2, 3))],
+            ("hinge", 14): [sine_planes(4, (0, 1))],
+            ("hinge", 15): [sine_planes(4, (2, 3))],
         }
 
-        def prepare(step):
+        def prepare(step, with_season):
             if step[0] == "hinge":
                 if step not in banks:
                     differences(step[1])
@@ -277,21 +291,24 @@ def tile_changepointtrendtimeslearnedsines_kernel(
                 c = chunk_of[g]
                 if (g, h) not in trend_sb and ("a", c) in quantised and ("delta", h) in quantised:
                     trend(g, h)
-                if ("season", g, h) not in banks and ("f", c) in quantised and ("beta", h) in quantised:
+                if with_season and ("season", g, h) not in banks and ("f", c) in quantised and ("beta", h) in quantised:
                     season(g, h)
 
         for k, step in enumerate(steps):
             for job in side.get(step, []):
                 job()
-            ahead = [later for later in steps[k + 1 :] if later[0] in ("hinge", "out")][:LEAD]
-            for later in [step] + ahead:
-                prepare(later)
+            for later in [step] + [later for later in steps[k + 1 :] if later[0] in ("hinge", "out")][:LEAD]:
+                prepare(later, True)
+            for later in [later for later in steps[k + 1 :] if later[0] == "out"][:TREND_LEAD]:
+                prepare(later, False)
             if step[0] == "hinge":
                 hinge(step[1])
             elif step[0] == "out":
                 finish(step[1], step[2])
             elif step[0] == "interleave":
-                interleave(nc.vector.tensor_copy, step[1:], delta_planes)
+                interleave(nc.vector.tensor_copy, ("delta", 1), delta_planes)
+            elif step[0] == "widen":
+                widen_first_half()
             else:
                 quantise(step[1:])
                 if step[1] == "f" and step[2] + 1 < n_chunks:

@@ -1,3 +1,4 @@
+import math
 from contextlib import ExitStack
 
 import concourse.mybir as mybir
@@ -19,8 +20,12 @@ PACK = 4
 HALF = 512
 TIME_ROW = 64
 CHUNK_TILES = (2, 3, 4, 4, 3)
-LEAD = 2
-TREND_LEAD = 4
+LEAD = 4
+SHARED = ("out", 99, 0)
+SPLIT = 256
+SBANKS = 3
+SLEAD = 2
+OFFSET = 0
 EARLY_TILES = 5
 ONE_PAIR = 0x3F803F80
 MINUS_ONE_PAIR = 0xBF80BF80
@@ -46,7 +51,7 @@ def tile_changepointtrendtimeslearnedsines_kernel(
         stationary = keep.tile([P, (PACK + 1) * P], BF16, name="stationary")
         nc.vector.memset(moving_early[:].bitcast(U32), MINUS_ONE_PAIR)
         nc.vector.memset(stationary[:].bitcast(U32), 0)
-        nc.vector.memset(stationary[TIME_ROW : TIME_ROW + 1, :].bitcast(U32), ONE_PAIR)
+        nc.vector.memset(stationary[TIME_ROW : TIME_ROW + 1, : PACK * P].bitcast(U32), ONE_PAIR)
         nc.vector.memset(moving_late[:].bitcast(U32), MINUS_ONE_PAIR)
 
         def moving(lo, hi):
@@ -77,14 +82,22 @@ def tile_changepointtrendtimeslearnedsines_kernel(
                 out=beta_raw[h][:], in_=beta[:, h * HALF : (h + 1) * HALF].rearrange("(p j) n -> p j n", j=PACK)
             )
 
-        nc.scalar.dma_start(out=s_row[:], in_=s.rearrange("(o k) -> o k", o=1))
-        nc.scalar.dma_start(out=omega_bf[:], in_=omega.rearrange("(p j) -> p j", j=PACK))
-        nc.scalar.dma_start(out=rho_bf[:], in_=rho.rearrange("(p j) -> p j", j=PACK))
-        nc.scalar.dma_start(out=amp_bf[:], in_=amp.rearrange("(p j) -> p j", j=PACK))
         nc.sync.dma_start(out=scale[:], in_=delta_scale.rearrange("(p j) o -> p (j o)", j=PACK))
-        nc.sync.dma_start(out=moving_early[TIME_ROW : TIME_ROW + 1, :], in_=t_row[:, :early])
         load_delta(0)
-        load_beta(0)
+        nc.scalar.dma_start(out=omega_bf[:], in_=omega.rearrange("(p j) -> p j", j=PACK))
+        nc.scalar.dma_start(out=s_row[:], in_=s.rearrange("(o k) -> o k", o=1))
+        nc.scalar.dma_start(out=moving_early[TIME_ROW : TIME_ROW + 1, :], in_=t_row[:, :early])
+        nc.scalar.dma_start(
+            out=beta_raw[0][:], in_=beta[:, :HALF].rearrange("(p j) n -> p j n", j=PACK)
+        )
+        nc.sync.dma_start(out=rho_bf[:], in_=rho.rearrange("(p j) -> p j", j=PACK))
+        nc.sync.dma_start(out=amp_bf[:], in_=amp.rearrange("(p j) -> p j", j=PACK))
+        nc.scalar.activation(
+            out=stationary[TIME_ROW : TIME_ROW + 1, PACK * P :],
+            in_=stationary[TIME_ROW : TIME_ROW + 1, PACK * P :],
+            func=ACT.Sin,
+            bias=math.pi / 2,
+        )
         nc.sync.dma_start(out=moving_late[TIME_ROW : TIME_ROW + 1, :], in_=t_row[:, early:])
         load_delta(1)
         load_beta(1)
@@ -92,14 +105,14 @@ def tile_changepointtrendtimeslearnedsines_kernel(
         omega_f32 = keep.tile([P, PACK], F32, name="omega_f32")
         amp_f32 = keep.tile([P, PACK], F32, name="amp_f32")
         nc.vector.tensor_copy(out=omega_f32[:], in_=omega_bf[:])
-        nc.vector.tensor_copy(
-            out=stationary[0:1, : PACK * P].rearrange("o (j m) -> o j m", j=PACK),
-            in_=s_row[:].rearrange("o (m j) -> o j m", j=PACK),
-        )
         scale_run = keep.tile([P, P * PACK], F32, name="scale_run")
         nc.vector.tensor_copy(
             out=scale_run[:].rearrange("p (n j) -> p n j", j=PACK),
             in_=scale[:].unsqueeze(1).to_broadcast([P, P, PACK]),
+        )
+        nc.vector.tensor_copy(
+            out=stationary[0:1, : PACK * P].rearrange("o (j m) -> o j m", j=PACK),
+            in_=s_row[:].rearrange("o (m j) -> o j m", j=PACK),
         )
 
         grouped = {}
@@ -120,21 +133,17 @@ def tile_changepointtrendtimeslearnedsines_kernel(
             nc.vector.quantize_mx(out=codes[:].bitcast(FP8X4), scales=scales[:], in_=grouped[key][:])
             quantised[key] = (codes, scales)
 
-        def interleave(engine_copy, key, planes):
-            dst = grouped_tile(key, HALF, keep, "grouped_%s%d" % key)
+        def interleave(engine_copy, key, planes, lo=0, hi=HALF):
+            if key not in grouped:
+                grouped_tile(key, HALF, keep, "grouped_%s%d" % key)
             engine_copy(
-                out=dst.rearrange("p (c i) j -> p c j i", i=4),
-                in_=planes[:].rearrange("p j (c i) -> p c j i", i=4),
+                out=grouped[key][:, lo * PACK : hi * PACK].rearrange("p (c i j) -> p c j i", i=4, j=PACK),
+                in_=planes[:, :, lo:hi].rearrange("p j (c i) -> p c j i", i=4),
             )
 
         def sine_plane(c, j):
             width = CHUNK_TILES[c] * P
             if j == 0:
-                times[c] = psum.tile([P, HALF], F32, name="times", tag="scalar_bank", bufs=3)
-                lo = first_tile[c] * P
-                nc.tensor.matmul(
-                    times[c][:, :width], lhsT=stationary[:, PACK * P :], rhs=moving(lo, lo + width), start=True, stop=True
-                )
                 sines[c] = work.tile([P, PACK, width], F32, name="sines", tag="sines", bufs=2)
             nc.scalar.activation(
                 out=sines[c][:, j, :], in_=times[c][:, :width], func=ACT.Sin, scale=omega_f32[:, j : j + 1]
@@ -152,9 +161,9 @@ def tile_changepointtrendtimeslearnedsines_kernel(
 
         def new_bank(key):
             if key[0] == "trend":
-                banks[key] = psum.tile([P, HALF], F32, name="bank", tag="scalar_bank", bufs=3)
+                banks[key] = psum.tile([P, HALF], F32, name="bank", tag="scalar_bank", bufs=SBANKS)
             else:
-                banks[key] = psum.tile([P, HALF], F32, name="bank", tag="vector_bank", bufs=5)
+                banks[key] = psum.tile([P, HALF], F32, name="bank", tag="vector_bank", bufs=8 - SBANKS)
             return banks[key]
 
         def differences(g):
@@ -200,25 +209,35 @@ def tile_changepointtrendtimeslearnedsines_kernel(
             )
             return bank
 
-        def trend(g, h):
-            bank = product("trend", "a", "delta", g, h)
-            trend_sb[(g, h)] = work.tile([P, HALF], F32, name="trend_sb", tag="trend_sb", bufs=TREND_LEAD + 2)
-            nc.scalar.copy(out=trend_sb[(g, h)][:], in_=bank[:])
+        def copy_trend(g, h):
+            trend_sb[(g, h)] = work.tile([P, HALF], F32, name="trend_sb", tag="trend_sb", bufs=10)
+            nc.scalar.copy(out=trend_sb[(g, h)][:], in_=banks[("trend", g, h)][:])
+
+        def spread_times(c):
+            width = CHUNK_TILES[c] * P
+            times[c] = psum.tile([P, HALF], F32, name="times", tag="scalar_bank", bufs=SBANKS)
+            lo = first_tile[c] * P
+            nc.tensor.matmul(
+                times[c][:, :width], lhsT=stationary[:, PACK * P :], rhs=moving(lo, lo + width), start=True, stop=True
+            )
 
         def season(g, h):
             product("season", "f", "beta", g, h)
 
-        def finish(g, h):
-            result = work.tile([P, HALF], F32, name="result", tag="result", bufs=6)
-            nc.vector.scalar_tensor_tensor(
-                out=result[:],
-                in0=banks[("season", g, h)][:],
-                scalar=1.0,
-                in1=trend_sb[(g, h)][:],
-                op0=ALU.add,
-                op1=ALU.mult,
-            )
-            nc.sync.dma_start(out=out[g * P : (g + 1) * P, h * HALF : (h + 1) * HALF], in_=result[:])
+        def finish(g, h, pieces):
+            width = HALF // pieces
+            for lo in range(0, HALF, width):
+                result = work.tile([P, width], F32, name="result", tag="result", bufs=6)
+                nc.vector.scalar_tensor_tensor(
+                    out=result[:],
+                    in0=banks[("season", g, h)][:, lo : lo + width],
+                    scalar=1.0,
+                    in1=trend_sb[(g, h)][:, lo : lo + width],
+                    op0=ALU.add,
+                    op1=ALU.mult,
+                )
+                col = h * HALF + lo
+                nc.sync.dma_start(out=out[g * P : (g + 1) * P, col : col + width], in_=result[:])
 
         def widen_first_half():
             grouped_tile(("delta", 0), HALF, keep, "grouped_delta0")
@@ -255,61 +274,70 @@ def tile_changepointtrendtimeslearnedsines_kernel(
         def q(*keys):
             return [("quantise",) + key for key in keys]
 
-        o1, o2, o3, o4 = outs(1), outs(2), outs(3), outs(4)
-        steps = (
-            [("widen",)] + hinges(0, 5)
-            + q(("delta", 0), ("a", 0), ("beta", 0), ("a", 1), ("f", 0))
-            + hinges(5, 7) + [("out", 0, 0)] + hinges(7, 9) + [("out", 1, 0)] + hinges(9, 11)
-            + q(("a", 2), ("delta", 1), ("beta", 1), ("f", 1))
-            + hinges(11, 13) + [("out", 0, 1), ("out", 1, 1)] + o1
-            + q(("a", 3), ("f", 2))
-            + hinges(13, 14) + o2[:3] + hinges(14, 15) + o2[3:6] + hinges(15, 16) + o2[6:7]
-            + q(("a", 4), ("f", 3))
-            + o2[7:] + o3[:-1]
-            + q(("f", 4))
-            + o3[-1:] + o4
-        )
-        side = {
-            ("widen",): [sine_planes(0, range(PACK))],
-            ("hinge", 0): [lambda: interleave(nc.scalar.copy, ("beta", 0), beta_raw[0]), sine_planes(1, range(PACK)), widen_second_half],
-            ("hinge", 5): [lambda: interleave(nc.scalar.copy, ("delta", 1), delta_planes)],
-            ("hinge", 7): [lambda: interleave(nc.scalar.copy, ("beta", 1), beta_raw[1])],
-            ("hinge", 9): [sine_planes(2, range(PACK))],
-            ("out", 2, 1): [sine_planes(3, (0,))],
-            ("out", 3, 0): [sine_planes(3, (1,))],
-            ("out", 4, 0): [sine_planes(3, (2, 3))],
-            ("hinge", 14): [sine_planes(4, (0, 1))],
-            ("hinge", 15): [sine_planes(4, (2, 3))],
-        }
+        def planes(c):
+            return [("sine", c, j) for j in range(PACK)]
 
-        def prepare(step, with_season):
-            if step[0] == "hinge":
-                if step not in banks:
-                    differences(step[1])
-            if step[0] == "out":
-                g, h = step[1:]
-                c = chunk_of[g]
-                if (g, h) not in trend_sb and ("a", c) in quantised and ("delta", h) in quantised:
-                    trend(g, h)
-                if with_season and ("season", g, h) not in banks and ("f", c) in quantised and ("beta", h) in quantised:
-                    season(g, h)
+        def staggered(keys, ahead):
+            seq = []
+            for key, later in zip(keys, ahead + [None] * len(keys)):
+                if later:
+                    seq.append(("copy",) + later[1:])
+                seq.append(key)
+            return seq
+
+        def copy(key):
+            return [("copy",) + key[1:]]
+
+        o0, o1, o2, o3, o4 = outs(0), outs(1), outs(2), outs(3), outs(4)
+        steps = (
+            planes(0) + [("widen0",), ("interleave", "beta", 0)] + hinges(0, 3) + planes(1) + hinges(3, 5) + [("widen",)]
+            + q(("delta", 0), ("a", 0), ("beta", 0), ("a", 1), ("f", 0))
+            + hinges(5, 6) + copy(o0[0]) + hinges(6, 7) + copy(o0[2]) + [o0[0], ("interleave", "delta", 1)] + hinges(7, 8) + [o0[2]]
+            + hinges(8, 9) + [("interleave", "beta", 1)] + hinges(9, 12) + planes(2)[:1] + hinges(12, 13) + planes(2)[1:]
+            + q(("delta", 1), ("a", 2), ("beta", 1), ("f", 1))
+            + copy(o0[1]) + hinges(13, 14) + staggered([o0[1], o0[3]] + o1, [o0[3]] + o1)
+            + planes(3) + q(("f", 2), ("a", 3))
+            + hinges(14, 15) + copy(o2[0]) + hinges(15, 16) + staggered(o2, o2[1:])
+            + planes(4) + q(("f", 3), ("a", 4))
+            + copy(o3[0]) + staggered(o3[:6], o3[1:7]) + q(("f", 4)) + staggered(o3[6:] + o4, o3[7:] + o4)
+        )
+
+        def feed(item):
+            if item[0] == "hinge" and item not in banks:
+                differences(item[1])
+            if item[0] == "sine" and item[1] not in times:
+                spread_times(item[1])
+            if item[0] in ("out", "copy"):
+                name, feature, weight = ("season", "f", "beta") if item[0] == "out" else ("trend", "a", "delta")
+                g, h = item[1:]
+                if (name, g, h) not in banks:
+                    if (feature, chunk_of[g]) not in quantised or (weight, h) not in quantised:
+                        return False
+                    product(name, feature, weight, g, h)
+            return True
+
+        def run_job(job):
+            if job[0] == "sine":
+                sine_plane(job[1], job[2])
+            elif job[0] == "copy":
+                copy_trend(job[1], job[2])
+            elif job[0] == "widen":
+                widen_second_half()
+            else:
+                interleave(nc.scalar.copy, job[1:], delta_planes if job[1] == "delta" else beta_raw[job[2]])
 
         for k, step in enumerate(steps):
-            for job in side.get(step, []):
-                job()
-            for later in [step] + [later for later in steps[k + 1 :] if later[0] in ("hinge", "out")][:LEAD]:
-                prepare(later, True)
-            for later in [later for later in steps[k + 1 :] if later[0] == "out"][:TREND_LEAD]:
-                prepare(later, False)
+            for later in steps[k : k + LEAD + 1]:
+                feed(later)
             if step[0] == "hinge":
                 hinge(step[1])
             elif step[0] == "out":
-                finish(step[1], step[2])
-            elif step[0] == "interleave":
-                interleave(nc.vector.tensor_copy, ("delta", 1), delta_planes)
-            elif step[0] == "widen":
+                finish(step[1], step[2], 2 if k + 1 == len(steps) else 1)
+            elif step[0] == "widen0":
                 widen_first_half()
-            else:
+            elif step[0] == "quantise":
                 quantise(step[1:])
                 if step[1] == "f" and step[2] + 1 < n_chunks:
                     amplitude(step[2] + 1)
+            else:
+                run_job(step)

import math
from contextlib import ExitStack

import concourse.mybir as mybir

T, K, N = 2048, 512, 1024
FLOPS = 2 * 2 * T * K * N

F32 = mybir.dt.float32
BF16 = mybir.dt.bfloat16
U32 = mybir.dt.uint32
U8 = mybir.dt.uint8
FP8 = mybir.dt.float8_e4m3fn
FP8X4 = mybir.dt.float8_e4m3fn_x4
ALU = mybir.AluOpType
ACT = mybir.ActivationFunctionType

P = 128
PACK = 4
HALF = 512
TIME_ROW = 64
CHUNK_TILES = (2, 3, 4, 4, 3)
LEAD = 4
SHARED = ("out", 99, 0)
SPLIT = 256
SBANKS = 3
SLEAD = 2
OFFSET = 0
EARLY_TILES = 5
ONE_PAIR = 0x3F803F80
MINUS_ONE_PAIR = 0xBF80BF80


def tile_changepointtrendtimeslearnedsines_kernel(
    tc, t, s, rho, delta_bytes, delta_scale, omega, amp, beta, out
):
    nc = tc.nc
    n_chunks = len(CHUNK_TILES)
    first_tile = [sum(CHUNK_TILES[:c]) for c in range(n_chunks)]
    chunk_of = [c for c in range(n_chunks) for unused in range(CHUNK_TILES[c])]

    with ExitStack() as ctx:
        keep = ctx.enter_context(tc.tile_pool(name="keep", bufs=1))
        work = ctx.enter_context(tc.tile_pool(name="work", bufs=1))
        psum = ctx.enter_context(tc.psum_pool(name="psum", bufs=1))
        ctx.enter_context(tc.manual_schedule())

        early = EARLY_TILES * P
        moving_early = keep.tile([P, early], BF16, name="moving_early")
        moving_late = keep.tile([P, T - early], BF16, name="moving_late")
        stationary = keep.tile([P, (PACK + 1) * P], BF16, name="stationary")
        nc.vector.memset(moving_early[:].bitcast(U32), MINUS_ONE_PAIR)
        nc.vector.memset(stationary[:].bitcast(U32), 0)
        nc.vector.memset(stationary[TIME_ROW : TIME_ROW + 1, : PACK * P].bitcast(U32), ONE_PAIR)
        nc.vector.memset(moving_late[:].bitcast(U32), MINUS_ONE_PAIR)

        def moving(lo, hi):
            return moving_early[:, lo:hi] if hi <= early else moving_late[:, lo - early : hi - early]

        s_row = keep.tile([1, K], BF16, name="s_row")
        omega_bf = keep.tile([P, PACK], BF16, name="omega_bf")
        rho_bf = keep.tile([P, PACK], BF16, name="rho_bf")
        amp_bf = keep.tile([P, PACK], BF16, name="amp_bf")
        scale = keep.tile([P, PACK], F32, name="scale")
        t_row = t.rearrange("(o i) -> o i", o=1)
        beta_raw = []
        delta_raw = []
        for h in range(2):
            raw = keep.tile([P, PACK, HALF], BF16, name="beta_raw%d" % h)
            beta_raw.append(raw)
            raw_bytes = keep.tile([P, PACK, HALF], U8, name="delta_raw%d" % h)
            delta_raw.append(raw_bytes)

        def load_delta(h):
            nc.sync.dma_start(
                out=delta_raw[h][:],
                in_=delta_bytes[:, h * HALF : (h + 1) * HALF].rearrange("(p j) n -> p j n", j=PACK),
            )

        def load_beta(h):
            nc.sync.dma_start(
                out=beta_raw[h][:], in_=beta[:, h * HALF : (h + 1) * HALF].rearrange("(p j) n -> p j n", j=PACK)
            )

        nc.sync.dma_start(out=scale[:], in_=delta_scale.rearrange("(p j) o -> p (j o)", j=PACK))
        load_delta(0)
        nc.scalar.dma_start(out=omega_bf[:], in_=omega.rearrange("(p j) -> p j", j=PACK))
        nc.scalar.dma_start(out=s_row[:], in_=s.rearrange("(o k) -> o k", o=1))
        nc.scalar.dma_start(out=moving_early[TIME_ROW : TIME_ROW + 1, :], in_=t_row[:, :early])
        nc.scalar.dma_start(
            out=beta_raw[0][:], in_=beta[:, :HALF].rearrange("(p j) n -> p j n", j=PACK)
        )
        nc.sync.dma_start(out=rho_bf[:], in_=rho.rearrange("(p j) -> p j", j=PACK))
        nc.sync.dma_start(out=amp_bf[:], in_=amp.rearrange("(p j) -> p j", j=PACK))
        nc.scalar.activation(
            out=stationary[TIME_ROW : TIME_ROW + 1, PACK * P :],
            in_=stationary[TIME_ROW : TIME_ROW + 1, PACK * P :],
            func=ACT.Sin,
            bias=math.pi / 2,
        )
        nc.sync.dma_start(out=moving_late[TIME_ROW : TIME_ROW + 1, :], in_=t_row[:, early:])
        load_delta(1)
        load_beta(1)

        omega_f32 = keep.tile([P, PACK], F32, name="omega_f32")
        amp_f32 = keep.tile([P, PACK], F32, name="amp_f32")
        nc.vector.tensor_copy(out=omega_f32[:], in_=omega_bf[:])
        scale_run = keep.tile([P, P * PACK], F32, name="scale_run")
        nc.vector.tensor_copy(
            out=scale_run[:].rearrange("p (n j) -> p n j", j=PACK),
            in_=scale[:].unsqueeze(1).to_broadcast([P, P, PACK]),
        )
        nc.vector.tensor_copy(
            out=stationary[0:1, : PACK * P].rearrange("o (j m) -> o j m", j=PACK),
            in_=s_row[:].rearrange("o (m j) -> o j m", j=PACK),
        )

        grouped = {}
        quantised = {}
        sines = {}
        times = {}
        banks = {}
        trend_sb = {}

        def grouped_tile(key, width, pool, tag):
            grouped[key] = pool.tile([P, width * PACK], BF16, name="grouped_%s%d" % key, tag=tag, align_bytes=64)
            return grouped[key][:].rearrange("p (n j) -> p n j", j=PACK)

        def quantise(key):
            width = grouped[key].shape[1] // PACK
            codes = keep.tile([P, width], U32, name="codes_%s%d" % key, align_bytes=64)
            scales = keep.tile([P, width], U8, name="scales_%s%d" % key, align_bytes=64)
            nc.vector.quantize_mx(out=codes[:].bitcast(FP8X4), scales=scales[:], in_=grouped[key][:])
            quantised[key] = (codes, scales)

        def interleave(engine_copy, key, planes, lo=0, hi=HALF):
            if key not in grouped:
                grouped_tile(key, HALF, keep, "grouped_%s%d" % key)
            engine_copy(
                out=grouped[key][:, lo * PACK : hi * PACK].rearrange("p (c i j) -> p c j i", i=4, j=PACK),
                in_=planes[:, :, lo:hi].rearrange("p j (c i) -> p c j i", i=4),
            )

        def sine_plane(c, j):
            width = CHUNK_TILES[c] * P
            if j == 0:
                sines[c] = work.tile([P, PACK, width], F32, name="sines", tag="sines", bufs=2)
            nc.scalar.activation(
                out=sines[c][:, j, :], in_=times[c][:, :width], func=ACT.Sin, scale=omega_f32[:, j : j + 1]
            )

        def amplitude(c):
            width = CHUNK_TILES[c] * P
            dst = grouped_tile(("f", c), width, work, "grouped_f")
            nc.gpsimd.tensor_tensor(
                out=dst.rearrange("p (c i) j -> p c j i", i=4),
                in0=sines[c][:].rearrange("p j (c i) -> p c j i", i=4),
                in1=amp_f32[:].unsqueeze(1).unsqueeze(3).to_broadcast([P, width // 4, PACK, 4]),
                op=ALU.mult,
            )

        def new_bank(key):
            if key[0] == "trend":
                banks[key] = psum.tile([P, HALF], F32, name="bank", tag="scalar_bank", bufs=SBANKS)
            else:
                banks[key] = psum.tile([P, HALF], F32, name="bank", tag="vector_bank", bufs=8 - SBANKS)
            return banks[key]

        def differences(g):
            bank = new_bank(("hinge", g))
            planes = bank[:].rearrange("p (i j) -> p j i", j=PACK)
            for j in range(PACK):
                nc.tensor.matmul(
                    planes[:, j, :],
                    lhsT=stationary[:, j * P : (j + 1) * P],
                    rhs=moving(g * P, (g + 1) * P),
                    start=True,
                    stop=True,
                )

        def hinge(g):
            c = chunk_of[g]
            if g == first_tile[c]:
                grouped_tile(("a", c), CHUNK_TILES[c] * P, keep, "grouped_a%d" % c)
            lo = (g - first_tile[c]) * P * PACK
            nc.vector.scalar_tensor_tensor(
                out=grouped[("a", c)][:, lo : lo + P * PACK].rearrange("p (i j) -> p i j", j=PACK),
                in0=banks[("hinge", g)][:].rearrange("p (i j) -> p i j", j=PACK),
                scalar=0.0,
                in1=rho_bf[:].unsqueeze(1).to_broadcast([P, P, PACK]),
                op0=ALU.max,
                op1=ALU.mult,
            )

        def product(name, feature, weight, g, h):
            c = chunk_of[g]
            cols = slice((g - first_tile[c]) * P, (g - first_tile[c] + 1) * P)
            codes, scales = quantised[(feature, c)]
            w_codes, w_scales = quantised[(weight, h)]
            bank = new_bank((name, g, h))
            nc.tensor.matmul_mx(
                bank[:],
                lhsT=codes[:, cols].bitcast(FP8X4),
                lhsT_scale=scales[:, cols],
                rhs=w_codes[:].bitcast(FP8X4),
                rhs_scale=w_scales[:],
                start=True,
                stop=True,
            )
            return bank

        def copy_trend(g, h):
            trend_sb[(g, h)] = work.tile([P, HALF], F32, name="trend_sb", tag="trend_sb", bufs=10)
            nc.scalar.copy(out=trend_sb[(g, h)][:], in_=banks[("trend", g, h)][:])

        def spread_times(c):
            width = CHUNK_TILES[c] * P
            times[c] = psum.tile([P, HALF], F32, name="times", tag="scalar_bank", bufs=SBANKS)
            lo = first_tile[c] * P
            nc.tensor.matmul(
                times[c][:, :width], lhsT=stationary[:, PACK * P :], rhs=moving(lo, lo + width), start=True, stop=True
            )

        def season(g, h):
            product("season", "f", "beta", g, h)

        def finish(g, h, pieces):
            width = HALF // pieces
            for lo in range(0, HALF, width):
                result = work.tile([P, width], F32, name="result", tag="result", bufs=6)
                nc.vector.scalar_tensor_tensor(
                    out=result[:],
                    in0=banks[("season", g, h)][:, lo : lo + width],
                    scalar=1.0,
                    in1=trend_sb[(g, h)][:, lo : lo + width],
                    op0=ALU.add,
                    op1=ALU.mult,
                )
                col = h * HALF + lo
                nc.sync.dma_start(out=out[g * P : (g + 1) * P, col : col + width], in_=result[:])

        def widen_first_half():
            grouped_tile(("delta", 0), HALF, keep, "grouped_delta0")
            for lo in range(0, HALF, P):
                nc.vector.tensor_tensor(
                    out=grouped[("delta", 0)][:, lo * PACK : (lo + P) * PACK].rearrange("p (n j) -> p n j", j=PACK),
                    in0=delta_raw[0][:, :, lo : lo + P].bitcast(FP8).rearrange("p j n -> p n j"),
                    in1=scale_run[:].rearrange("p (n j) -> p n j", j=PACK),
                    op=ALU.mult,
                )
            nc.vector.tensor_copy(out=amp_f32[:], in_=amp_bf[:])
            amplitude(0)

        delta_planes = keep.tile([P, PACK, HALF], BF16, name="delta_planes")

        def widen_second_half():
            for j in range(PACK):
                nc.scalar.activation(
                    out=delta_planes[:, j, :],
                    in_=delta_raw[1][:, j, :].bitcast(FP8),
                    func=ACT.Copy,
                    scale=scale[:, j : j + 1],
                )

        def sine_planes(c, planes):
            return lambda: [sine_plane(c, j) for j in planes]

        def outs(c):
            return [("out", g, h) for g in range(first_tile[c], first_tile[c] + CHUNK_TILES[c]) for h in range(2)]

        def hinges(lo, hi):
            return [("hinge", g) for g in range(lo, hi)]

        def q(*keys):
            return [("quantise",) + key for key in keys]

        def planes(c):
            return [("sine", c, j) for j in range(PACK)]

        def staggered(keys, ahead):
            seq = []
            for key, later in zip(keys, ahead + [None] * len(keys)):
                if later:
                    seq.append(("copy",) + later[1:])
                seq.append(key)
            return seq

        def copy(key):
            return [("copy",) + key[1:]]

        o0, o1, o2, o3, o4 = outs(0), outs(1), outs(2), outs(3), outs(4)
        steps = (
            planes(0) + [("widen0",), ("interleave", "beta", 0)] + hinges(0, 3) + planes(1) + hinges(3, 5) + [("widen",)]
            + q(("delta", 0), ("a", 0), ("beta", 0), ("a", 1), ("f", 0))
            + hinges(5, 6) + copy(o0[0]) + hinges(6, 7) + copy(o0[2]) + [o0[0], ("interleave", "delta", 1)] + hinges(7, 8) + [o0[2]]
            + hinges(8, 9) + [("interleave", "beta", 1)] + hinges(9, 12) + planes(2)[:1] + hinges(12, 13) + planes(2)[1:]
            + q(("delta", 1), ("a", 2), ("beta", 1), ("f", 1))
            + copy(o0[1]) + hinges(13, 14) + staggered([o0[1], o0[3]] + o1, [o0[3]] + o1)
            + planes(3) + q(("f", 2), ("a", 3))
            + hinges(14, 15) + copy(o2[0]) + hinges(15, 16) + staggered(o2, o2[1:])
            + planes(4) + q(("f", 3), ("a", 4))
            + copy(o3[0]) + staggered(o3[:6], o3[1:7]) + q(("f", 4)) + staggered(o3[6:] + o4, o3[7:] + o4)
        )

        def feed(item):
            if item[0] == "hinge" and item not in banks:
                differences(item[1])
            if item[0] == "sine" and item[1] not in times:
                spread_times(item[1])
            if item[0] in ("out", "copy"):
                name, feature, weight = ("season", "f", "beta") if item[0] == "out" else ("trend", "a", "delta")
                g, h = item[1:]
                if (name, g, h) not in banks:
                    if (feature, chunk_of[g]) not in quantised or (weight, h) not in quantised:
                        return False
                    product(name, feature, weight, g, h)
            return True

        def run_job(job):
            if job[0] == "sine":
                sine_plane(job[1], job[2])
            elif job[0] == "copy":
                copy_trend(job[1], job[2])
            elif job[0] == "widen":
                widen_second_half()
            else:
                interleave(nc.scalar.copy, job[1:], delta_planes if job[1] == "delta" else beta_raw[job[2]])

        for k, step in enumerate(steps):
            for later in steps[k : k + LEAD + 1]:
                feed(later)
            if step[0] == "hinge":
                hinge(step[1])
            elif step[0] == "out":
                finish(step[1], step[2], 2 if k + 1 == len(steps) else 1)
            elif step[0] == "widen0":
                widen_first_half()
            elif step[0] == "quantise":
                quantise(step[1:])
                if step[1] == "f" and step[2] + 1 < n_chunks:
                    amplitude(step[2] + 1)
            else:
                run_job(step)
